import numpy as np
import ml_dtypes


def mxq(x, axis, fmt="e4m3"):
    dtype, down = {"e4m3": (ml_dtypes.float8_e4m3fn, 7), "e5m2": (ml_dtypes.float8_e5m2, 14)}[fmt]
    v = np.moveaxis(np.asarray(x, np.float32).astype(ml_dtypes.bfloat16).astype(np.float64), axis, -1)
    blocks = v.reshape(v.shape[:-1] + (-1, 32))
    amax = np.abs(blocks).max(-1, keepdims=True)
    byte = np.maximum(np.where(amax > 0, np.frexp(amax)[1] - 1 + 127, 0) - down, 1)
    scale = np.exp2(byte - 127.0)
    codes = (blocks / scale).astype(np.float32).astype(dtype).astype(np.float64)
    return np.moveaxis((codes * scale).reshape(v.shape), -1, axis)


WIDE = False


def mx_kscale(k):
    if not WIDE:
        return np.ones(k)
    levels = np.array([10, -10, 5, -5, 0])
    if k % 512:
        return np.exp2(np.random.permutation(np.resize(levels, k // 32))).repeat(32)
    a = np.empty((k // 512, 16))
    for p in range(k // 512):
        a[p, :8] = np.random.permutation(np.resize(levels, 8))
        for g in range(8):
            far = levels[np.abs(levels - a[p, g]) >= 10]
            a[p, g + 8] = far[np.random.randint(len(far))]
    return np.exp2(a.ravel()).repeat(32)


def f64(x):
    return np.asarray(x).astype(np.float64)


def striped(idx):
    return np.tile(idx.reshape(-1, 16).T, (8, 1)).astype(np.uint16)


def unstriped(offs):
    return offs[:16].T.reshape(-1).astype(np.int64)


def striped8(idx):
    return np.concatenate([x.reshape(-1, 16).T for x in idx]).astype(np.uint16)


def runs(offs, k):
    lists = np.stack([offs[16 * r : 16 * r + 16].T.reshape(-1) for r in range(8)]).astype(np.int64)
    return lists[np.arange(k) % 512 // 64]


def pack_weight(w):
    k, n = w.shape
    w = f64(np.asarray(w, np.float32).astype(ml_dtypes.bfloat16)).reshape(k // 32, 32, n)
    amax = np.abs(w).max(1)
    byte = np.clip(np.where(amax > 0, np.frexp(amax)[1] - 1 + 127 - 7, 1), 1, 254)
    scaled = (w * np.exp2(127.0 - byte)[:, None, :]).reshape(k, n).astype(np.float32)
    words = np.ascontiguousarray(scaled.reshape(k // 512, 128, 4, n).transpose(0, 1, 3, 2)).astype(ml_dtypes.float8_e4m3fn).view(np.uint8)
    return words, np.ascontiguousarray(byte.astype(np.uint8).reshape(k // 512, 16, n))


def unpack_weight(words, scales):
    g, p, n, _ = words.shape
    vals = np.ascontiguousarray(words).view(ml_dtypes.float8_e4m3fn).astype(np.float64) * np.repeat(np.exp2(scales.astype(np.float64) - 127.0), 8, axis=1)[..., None]
    return vals.transpose(0, 1, 3, 2).reshape(g * 512, n)


def sigmoid(v):
    return 1.0 / (1.0 + np.exp(-np.maximum(v, -700.0)))


K, T, S, H, C = 512, 2048, 512, 512, 512


def setup_inputs():
    n = np.random.standard_normal
    s = mx_kscale(K)[:, None]
    packed_xT = pack_weight(n((K, T)) * s)
    return {
        "x_words": packed_xT[0],
        "x_scales": packed_xT[1],
        "w1": (n((K, H)) / np.sqrt(K) / s).astype(np.float32),
        "w2": (n((K, H)) / np.sqrt(K) / s).astype(np.float32),
        "gs": (np.random.uniform(0.5, 1.5, (K, 1)) / s).astype(np.float32),
        "offs": striped(np.random.permutation(T)[:S]),
        "two": striped(np.random.permutation(T)[:S]),
        "n1": striped8(np.stack([np.random.permutation(S) for _ in range(8)])),
        "n2": striped8(np.stack([np.random.permutation(S) for _ in range(8)])),
        "cand": striped(np.random.permutation(T)[:C]),
        "n3": striped8(np.stack([np.random.permutation(S) for _ in range(8)])),
        "n4": striped8(np.stack([np.random.permutation(S) for _ in range(8)])),
    }


def reference(x_words, x_scales, w1, w2, gs, offs, two, n1, n2, cand, n3, n4):
    x_cand = unpack_weight(x_words, x_scales)[:, unstriped(cand)]
    xq = unpack_weight(x_words, x_scales)[:, unstriped(offs)]
    y = mxq(f64(w1), 0, "e4m3").T @ xq
    x_two = unpack_weight(x_words, x_scales)[:, unstriped(two)]
    d = mxq(f64(w2), 0, "e4m3").T @ x_two
    z = f64(gs) * (y * (np.tanh(d[np.arange(H)[:, None], runs(n1, H)] - (d[np.arange(H)[:, None], runs(n2, H)]))))
    s = 0.0625 * ((x_cand.T @ mxq(z, 0, "e4m3")))
    return s + (sigmoid(s[np.arange(C)[:, None], runs(n3, C)])) * (s[np.arange(C)[:, None], runs(n4, C)] - s)

@@ -1,0 +1,203 @@
+from contextlib import ExitStack
+
+import concourse.mybir as mybir
+
+K, T, S, H, C = 512, 2048, 512, 512, 512
+FLOPS = 3 * 2 * 512 * 512 * 512
+
+F32 = mybir.dt.float32
+BF16 = mybir.dt.bfloat16
+I32 = mybir.dt.int32
+U32 = mybir.dt.uint32
+U16 = mybir.dt.uint16
+U8 = mybir.dt.uint8
+FP8X4 = mybir.dt.float8_e4m3fn_x4
+ACT = mybir.ActivationFunctionType
+ALU = mybir.AluOpType
+
+P = 128
+PACK = 4
+HALF = 256
+SCALAR_FETCH = (1, 2, 4, 5, 6)
+
+
+def tile_picked_twcjointbtrack_none_p_kernel(
+    tc, x_words, x_scales, w1, w2, gs, offs, two, n1, n2, cand, n3, n4, out
+):
+    nc = tc.nc
+    with ExitStack() as ctx:
+        keep = ctx.enter_context(tc.tile_pool(name="keep", bufs=1))
+        shared = ctx.enter_context(tc.tile_pool(name="shared", bufs=1))
+        ring = ctx.enter_context(tc.tile_pool(name="ring", bufs=3))
+        psum = ctx.enter_context(tc.psum_pool(name="psum", bufs=1))
+
+        lists = {}
+        for name in ("two", "offs", "n1", "n2", "cand", "n3", "n4"):
+            lists[name] = keep.tile([P, S // 16], U16, name="list_" + name)
+
+        def entries(name, h):
+            return lists[name][:, h * HALF // 16 : (h + 1) * HALF // 16]
+
+        xw = keep.tile([P, T], U32, name="xw", align_bytes=64)
+        xs = keep.tile([P, T], U8, name="xs", align_bytes=64)
+        gain = keep.tile([P, PACK], F32, name="gain")
+        nc.vector.memset(xs[:].bitcast(I32), 0)
+        nc.sync.dma_start(out=xw[:].bitcast(I32), in_=x_words[0].rearrange("p n r -> p (n r)").bitcast(I32))
+        for q in range(4):
+            nc.scalar.dma_start(
+                out=xs[32 * q : 32 * q + 4, :].bitcast(I32), in_=x_scales[0, 4 * q : 4 * q + 4, :].bitcast(I32)
+            )
+        nc.gpsimd.dma_start(out=gain[:], in_=gs.rearrange("(p t) o -> p (t o)", t=PACK))
+
+        def load_weight(w, name):
+            halves = []
+            for h in range(2):
+                raw = keep.tile([P, PACK, HALF], F32, name="%s_raw%d" % (name, h))
+                nc.sync.dma_start(
+                    out=raw[:], in_=w.rearrange("(p j) c -> p j c", j=PACK)[:, :, h * HALF : (h + 1) * HALF]
+                )
+                halves.append(raw)
+            return halves
+
+        nc.sync.dma_start(out=lists["two"][:], in_=two)
+        raw2 = load_weight(w2, "w2")
+        nc.sync.dma_start(out=lists["offs"][:], in_=offs)
+        raw1 = load_weight(w1, "w1")
+        nc.sync.dma_start(out=lists["n1"][:], in_=n1)
+        nc.sync.dma_start(out=lists["n2"][:], in_=n2)
+        nc.sync.dma_start(out=lists["cand"][:], in_=cand)
+        nc.sync.dma_start(out=lists["n3"][:], in_=n3)
+        nc.sync.dma_start(out=lists["n4"][:], in_=n4)
+
+        def pick(name, words, scales, dealt):
+            for dst, src in ((words, xw), (scales, xs)):
+                view = dst[:].rearrange("p (t m) -> p m t", t=PACK) if dealt else dst[:]
+                nc.vector.tensor_copy(out=view, in_=src[:].indirect(lists[name][:]))
+            return words, scales
+
+        def round_weight(grouped, halves, h):
+            m0 = h * HALF // PACK
+            nc.scalar.activation(
+                out=grouped[:, :, m0 : m0 + HALF // PACK, :].rearrange("p t m j -> p m t j"),
+                in_=halves[h][:].rearrange("p j (m t) -> p m t j", t=PACK),
+                func=ACT.Copy,
+            )
+
+        def quantise_weight(grouped, name):
+            words = keep.tile([P, H], U32, name=name + "_words", align_bytes=64)
+            scales = keep.tile([P, H], U8, name=name + "_scales", align_bytes=64)
+            flat = grouped[:].rearrange("p t m j -> p (t m j)")
+            for u in range(2):
+                nc.vector.quantize_mx(
+                    out=words[:, u * HALF : (u + 1) * HALF].bitcast(FP8X4),
+                    scales=scales[:, u * HALF : (u + 1) * HALF],
+                    in_=flat[:, u * PACK * HALF : (u + 1) * PACK * HALF],
+                )
+            return words, scales
+
+        def product(acc, stationary, t, moving):
+            nc.tensor.matmul_mx(
+                out=acc,
+                lhsT=stationary[0][:, t * P : (t + 1) * P].bitcast(FP8X4),
+                lhsT_scale=stationary[1][:, t * P : (t + 1) * P],
+                rhs=moving[0][:].bitcast(FP8X4),
+                rhs_scale=moving[1][:],
+                start=True,
+                stop=True,
+            )
+
+        x_two = pick(
+            "two",
+            keep.tile([P, S], U32, name="two_words", align_bytes=64),
+            keep.tile([P, S], U8, name="two_scales", align_bytes=64),
+            False,
+        )
+        grouped2 = shared.tile([P, PACK, P, PACK], BF16, name="w2_bf16", align_bytes=64, offset=0)
+        round_weight(grouped2, raw2, 0)
+        round_weight(grouped2, raw2, 1)
+        w2_mx = quantise_weight(grouped2, "w2")
+        x_offs = pick(
+            "offs",
+            keep.tile([P, S], U32, name="offs_words", align_bytes=64),
+            shared.tile([P, S], U8, name="offs_scales", align_bytes=64, offset=0),
+            False,
+        )
+        d_acc = []
+        d_rows = []
+        for t in range(PACK):
+            acc = psum.tile([P, S], F32, name="d_acc%d" % t, tag="bank%d" % t)
+            product(acc[:], w2_mx, t, x_two)
+            d_acc.append(acc)
+            d_rows.append(keep.tile([P, S], F32, name="d_rows%d" % t))
+        grouped1 = keep.tile([P, PACK, P, PACK], BF16, name="w1_bf16", align_bytes=64)
+        round_weight(grouped1, raw1, 0)
+        nc.scalar.activation(out=d_rows[0][:], in_=d_acc[0][:], func=ACT.Copy)
+        round_weight(grouped1, raw1, 1)
+        w1_mx = quantise_weight(grouped1, "w1")
+        x_cand = pick(
+            "cand",
+            shared.tile([P, S], U32, name="cand_words", align_bytes=64, offset=1024),
+            shared.tile([P, S], U8, name="cand_scales", align_bytes=64, offset=512),
+            True,
+        )
+        y_acc = []
+        for t in range(PACK):
+            acc = psum.tile([P, S], F32, name="y_acc%d" % t)
+            product(acc[:], w1_mx, t, x_offs)
+            y_acc.append(acc)
+
+        s_acc = [psum.tile([P, S], F32, name="s_acc%d" % t, tag="bank%d" % t) for t in range(PACK)]
+        s_rows = [keep.tile([P, S], F32, name="s_rows%d" % t) for t in range(PACK)]
+        for h in range(2):
+            cols = slice(h * HALF, (h + 1) * HALF)
+            z_planes = keep.tile([P, PACK, HALF], BF16, name="z_planes%d" % h)
+            for t in range(PACK):
+                if h == 0 and t > 0:
+                    nc.scalar.activation(out=d_rows[t][:], in_=d_acc[t][:], func=ACT.Copy)
+                d1 = ring.tile([P, HALF], F32, name="d1")
+                nc.scalar.activation(out=d1[:], in_=d_rows[t][:].indirect(entries("n1", h)), func=ACT.Copy)
+                gap = ring.tile([P, HALF], F32, name="gap")
+                nc.vector.tensor_tensor(gap[:], d_rows[t][:].indirect(entries("n2", h)), d1[:], ALU.subtract)
+                gate = ring.tile([P, HALF], F32, name="gate")
+                nc.scalar.activation(out=gate[:], in_=gap[:], func=ACT.Tanh, scale=-1.0)
+                nc.vector.scalar_tensor_tensor(
+                    z_planes[:, t, :], y_acc[t][:, cols], gain[:, t : t + 1], gate[:], ALU.mult, ALU.mult
+                )
+            z_grouped = keep.tile([P, HALF, PACK], BF16, name="z_grouped%d" % h, align_bytes=64)
+            nc.vector.tensor_copy(
+                out=z_grouped[:].rearrange("p (c i) t -> p c t i", i=4),
+                in_=z_planes[:].rearrange("p t (c i) -> p c t i", i=4),
+            )
+            z_words = keep.tile([P, HALF], U32, name="z_words%d" % h, align_bytes=64)
+            z_scales = keep.tile([P, HALF], U8, name="z_scales%d" % h, align_bytes=64)
+            nc.vector.quantize_mx(
+                out=z_words[:].bitcast(FP8X4), scales=z_scales[:], in_=z_grouped[:].rearrange("p n t -> p (n t)")
+            )
+            for t in range(PACK):
+                product(s_acc[t][:, cols], x_cand, t, (z_words, z_scales))
+                if h == 0 or t == 0:
+                    nc.scalar.activation(out=s_rows[t][:, cols], in_=s_acc[t][:, cols], func=ACT.Copy, scale=0.0625)
+                else:
+                    nc.vector.tensor_scalar(s_rows[t][:, cols], s_acc[t][:, cols], 0.0625, None, ALU.mult)
+
+        out_rows = out.rearrange("(p t) c -> p t c", t=PACK)
+        for t in range(PACK):
+            for h in range(2):
+                cols = slice(h * HALF, (h + 1) * HALF)
+                window = s_rows[t]
+                sig = ring.tile([P, HALF], F32, name="sig")
+                nc.scalar.activation(out=sig[:], in_=window[:].indirect(entries("n3", h)), func=ACT.Sigmoid)
+                first = ring.tile([P, HALF], F32, name="first")
+                second = ring.tile([P, HALF], F32, name="second")
+                result = ring.tile([P, HALF], F32, name="result", bufs=8)
+                if 2 * t + h in SCALAR_FETCH:
+                    s4 = ring.tile([P, HALF], F32, name="s4")
+                    nc.scalar.activation(out=s4[:], in_=window[:].indirect(entries("n4", h)), func=ACT.Copy)
+                    nc.vector.tensor_tensor(first[:], s4[:], window[:, cols], ALU.subtract)
+                    nc.vector.tensor_tensor(second[:], first[:], sig[:], ALU.mult)
+                    nc.vector.tensor_tensor(result[:], second[:], window[:, cols], ALU.add)
+                else:
+                    nc.vector.tensor_tensor(first[:], window[:].indirect(entries("n4", h)), sig[:], ALU.mult)
+                    nc.vector.scalar_tensor_tensor(second[:], sig[:], -1.0, window[:, cols], ALU.add, ALU.mult)
+                    nc.vector.tensor_tensor(result[:], first[:], second[:], ALU.subtract)
+                nc.sync.dma_start(out=out_rows[:, t, cols], in_=result[:])

@@ -18,7 +18,10 @@ ALU = mybir.AluOpType
 P = 128
 PACK = 4
 HALF = 256
-SCALAR_FETCH = (1, 2, 4, 5, 6)
+WINDOW = 1024
+GPSIMD_CHANNELS = 32
+SCALAR_WEAVE = 192
+PIECES = ((0, 0, 256, False), (0, 256, 512, False), (1, 0, 512, False), (2, 0, 512, True), (3, 0, 256, True), (3, 256, 512, True))
 
 
 def tile_picked_twcjointbtrack_none_p_kernel(
@@ -28,15 +31,11 @@ def tile_picked_twcjointbtrack_none_p_kernel(
     with ExitStack() as ctx:
         keep = ctx.enter_context(tc.tile_pool(name="keep", bufs=1))
         shared = ctx.enter_context(tc.tile_pool(name="shared", bufs=1))
-        ring = ctx.enter_context(tc.tile_pool(name="ring", bufs=3))
         psum = ctx.enter_context(tc.psum_pool(name="psum", bufs=1))
 
         lists = {}
         for name in ("two", "offs", "n1", "n2", "cand", "n3", "n4"):
             lists[name] = keep.tile([P, S // 16], U16, name="list_" + name)
-
-        def entries(name, h):
-            return lists[name][:, h * HALF // 16 : (h + 1) * HALF // 16]
 
         xw = keep.tile([P, T], U32, name="xw", align_bytes=64)
         xs = keep.tile([P, T], U8, name="xs", align_bytes=64)
@@ -44,10 +43,15 @@ def tile_picked_twcjointbtrack_none_p_kernel(
         nc.vector.memset(xs[:].bitcast(I32), 0)
         nc.sync.dma_start(out=xw[:].bitcast(I32), in_=x_words[0].rearrange("p n r -> p (n r)").bitcast(I32))
         for q in range(4):
-            nc.scalar.dma_start(
+            nc.sync.dma_start(
                 out=xs[32 * q : 32 * q + 4, :].bitcast(I32), in_=x_scales[0, 4 * q : 4 * q + 4, :].bitcast(I32)
             )
-        nc.gpsimd.dma_start(out=gain[:], in_=gs.rearrange("(p t) o -> p (t o)", t=PACK))
+        windows = [keep.tile([P, WINDOW], F32, name="window%d" % t) for t in range(PACK)]
+        for t in range(PACK):
+            nc.gpsimd.memset(windows[t][:, S:], 0.0)
+        warm = keep.tile([P, 2], F32, name="warm")
+        nc.gpsimd.memset(warm[:, 0:1], 0.0)
+        nc.scalar.activation(out=warm[:, 1:2], in_=warm[:, 0:1], func=ACT.Sigmoid)
 
         def load_weight(w, name):
             halves = []
@@ -66,6 +70,7 @@ def tile_picked_twcjointbtrack_none_p_kernel(
         nc.sync.dma_start(out=lists["n1"][:], in_=n1)
         nc.sync.dma_start(out=lists["n2"][:], in_=n2)
         nc.sync.dma_start(out=lists["cand"][:], in_=cand)
+        nc.sync.dma_start(out=gain[:], in_=gs.rearrange("(p t) o -> p (t o)", t=PACK))
         nc.sync.dma_start(out=lists["n3"][:], in_=n3)
         nc.sync.dma_start(out=lists["n4"][:], in_=n4)
 
@@ -75,25 +80,17 @@ def tile_picked_twcjointbtrack_none_p_kernel(
                 nc.vector.tensor_copy(out=view, in_=src[:].indirect(lists[name][:]))
             return words, scales
 
-        def round_weight(grouped, halves, h):
-            m0 = h * HALF // PACK
-            nc.scalar.activation(
-                out=grouped[:, :, m0 : m0 + HALF // PACK, :].rearrange("p t m j -> p m t j"),
-                in_=halves[h][:].rearrange("p j (m t) -> p m t j", t=PACK),
-                func=ACT.Copy,
-            )
+        def round_weight(on_scalar, grouped, halves, m0, m1):
+            h, base = divmod(m0, HALF // PACK)
+            dst = grouped[:, :, m0:m1, :].rearrange("p t m j -> p m t j")
+            src = halves[h][:].rearrange("p j (m t) -> p m t j", t=PACK)[:, base : base + m1 - m0]
+            if on_scalar:
+                nc.scalar.activation(out=dst, in_=src, func=ACT.Copy)
+            else:
+                nc.gpsimd.tensor_scalar(dst, src, 1.0, 0.0, ALU.mult, ALU.add)
 
-        def quantise_weight(grouped, name):
-            words = keep.tile([P, H], U32, name=name + "_words", align_bytes=64)
-            scales = keep.tile([P, H], U8, name=name + "_scales", align_bytes=64)
-            flat = grouped[:].rearrange("p t m j -> p (t m j)")
-            for u in range(2):
-                nc.vector.quantize_mx(
-                    out=words[:, u * HALF : (u + 1) * HALF].bitcast(FP8X4),
-                    scales=scales[:, u * HALF : (u + 1) * HALF],
-                    in_=flat[:, u * PACK * HALF : (u + 1) * PACK * HALF],
-                )
-            return words, scales
+        def quantise(flat, words, scales):
+            nc.vector.quantize_mx(out=words.bitcast(FP8X4), scales=scales, in_=flat)
 
         def product(acc, stationary, t, moving):
             nc.tensor.matmul_mx(
@@ -106,98 +103,132 @@ def tile_picked_twcjointbtrack_none_p_kernel(
                 stop=True,
             )
 
-        x_two = pick(
-            "two",
-            keep.tile([P, S], U32, name="two_words", align_bytes=64),
-            keep.tile([P, S], U8, name="two_scales", align_bytes=64),
-            False,
-        )
+        def mx_tiles(name, width):
+            return (
+                keep.tile([P, width], U32, name=name + "_words", align_bytes=64),
+                keep.tile([P, width], U8, name=name + "_scales", align_bytes=64),
+            )
+
+        x_two = pick("two", *mx_tiles("two", S), False)
         grouped2 = shared.tile([P, PACK, P, PACK], BF16, name="w2_bf16", align_bytes=64, offset=0)
-        round_weight(grouped2, raw2, 0)
-        round_weight(grouped2, raw2, 1)
-        w2_mx = quantise_weight(grouped2, "w2")
+        round_weight(True, grouped2, raw2, 0, 64)
+        round_weight(True, grouped2, raw2, 64, P - GPSIMD_CHANNELS)
+        round_weight(False, grouped2, raw2, P - GPSIMD_CHANNELS, P)
+        w2_mx = mx_tiles("w2", H)
+        flat2 = grouped2[:].rearrange("p t m j -> p (t m j)")
+        for u in range(2):
+            cols = slice(u * HALF, (u + 1) * HALF)
+            quantise(flat2[:, u * PACK * HALF : (u + 1) * PACK * HALF], w2_mx[0][:, cols], w2_mx[1][:, cols])
         x_offs = pick(
             "offs",
             keep.tile([P, S], U32, name="offs_words", align_bytes=64),
             shared.tile([P, S], U8, name="offs_scales", align_bytes=64, offset=0),
             False,
         )
-        d_acc = []
-        d_rows = []
-        for t in range(PACK):
-            acc = psum.tile([P, S], F32, name="d_acc%d" % t, tag="bank%d" % t)
-            product(acc[:], w2_mx, t, x_two)
-            d_acc.append(acc)
-            d_rows.append(keep.tile([P, S], F32, name="d_rows%d" % t))
-        grouped1 = keep.tile([P, PACK, P, PACK], BF16, name="w1_bf16", align_bytes=64)
-        round_weight(grouped1, raw1, 0)
-        nc.scalar.activation(out=d_rows[0][:], in_=d_acc[0][:], func=ACT.Copy)
-        round_weight(grouped1, raw1, 1)
-        w1_mx = quantise_weight(grouped1, "w1")
         x_cand = pick(
             "cand",
             shared.tile([P, S], U32, name="cand_words", align_bytes=64, offset=1024),
             shared.tile([P, S], U8, name="cand_scales", align_bytes=64, offset=512),
             True,
         )
-        y_acc = []
+        d_acc = [psum.tile([P, S], F32, name="d_acc%d" % t, tag="bank%d" % t) for t in range(PACK)]
         for t in range(PACK):
-            acc = psum.tile([P, S], F32, name="y_acc%d" % t)
-            product(acc[:], w1_mx, t, x_offs)
-            y_acc.append(acc)
+            product(d_acc[t][:], w2_mx, t, x_two)
+        grouped1 = shared.tile([P, PACK, P, PACK], BF16, name="w1_bf16", align_bytes=64, offset=3072)
+        round_weight(False, grouped1, raw1, 0, 64)
+        round_weight(False, grouped1, raw1, 64, P)
 
-        s_acc = [psum.tile([P, S], F32, name="s_acc%d" % t, tag="bank%d" % t) for t in range(PACK)]
-        s_rows = [keep.tile([P, S], F32, name="s_rows%d" % t) for t in range(PACK)]
+        y_acc = [psum.tile([P, S], F32, name="y_acc%d" % t, tag="bank%d" % (PACK + t)) for t in range(PACK)]
+        gaps = [keep.tile([P, S], F32, name="gap%d" % t) for t in range(PACK)]
+        z_planes = keep.tile([P, PACK, S], BF16, name="z_planes")
+
+        def difference(t):
+            nc.scalar.activation(out=windows[t][:, :S], in_=d_acc[t][:], func=ACT.Copy)
+            d1 = keep.tile([P, S], F32, name="d1_%d" % t)
+            nc.scalar.activation(out=d1[:], in_=windows[t][:].indirect(lists["n1"][:]), func=ACT.Copy)
+            nc.vector.tensor_tensor(gaps[t][:], windows[t][:].indirect(lists["n2"][:]), d1[:], ALU.subtract)
+
+        def gated(t):
+            gate = keep.tile([P, S], F32, name="gate%d" % t)
+            nc.scalar.activation(out=gate[:], in_=gaps[t][:], func=ACT.Tanh, scale=-1.0)
+            nc.vector.scalar_tensor_tensor(
+                z_planes[:, t, :], y_acc[t][:], gain[:, t : t + 1], gate[:], ALU.mult, ALU.mult
+            )
+
+        difference(0)
+        w1_mx = mx_tiles("w1", H)
+        quantise(grouped1[:].rearrange("p t m j -> p (t m j)"), w1_mx[0][:], w1_mx[1][:])
+        for t in range(PACK):
+            product(y_acc[t][:], w1_mx, t, x_offs)
+        difference(1)
+        difference(2)
+        gated(0)
+        difference(3)
+        for t in range(1, PACK):
+            gated(t)
+
+        z_grouped = keep.tile([P, S, PACK], BF16, name="z_grouped", align_bytes=64)
+
+        def weave(copy, c0, c1):
+            copy(
+                out=z_grouped[:, c0:c1, :].rearrange("p (c i) t -> p c t i", i=4),
+                in_=z_planes[:, :, c0:c1].rearrange("p t (c i) -> p c t i", i=4),
+            )
+
+        weave(nc.scalar.copy, S - SCALAR_WEAVE, S)
+        weave(nc.vector.tensor_copy, 0, HALF)
+        weave(nc.vector.tensor_copy, HALF, S - SCALAR_WEAVE)
+        z_mx = [mx_tiles("z%d" % h, HALF) for h in range(2)]
         for h in range(2):
             cols = slice(h * HALF, (h + 1) * HALF)
-            z_planes = keep.tile([P, PACK, HALF], BF16, name="z_planes%d" % h)
-            for t in range(PACK):
-                if h == 0 and t > 0:
-                    nc.scalar.activation(out=d_rows[t][:], in_=d_acc[t][:], func=ACT.Copy)
-                d1 = ring.tile([P, HALF], F32, name="d1")
-                nc.scalar.activation(out=d1[:], in_=d_rows[t][:].indirect(entries("n1", h)), func=ACT.Copy)
-                gap = ring.tile([P, HALF], F32, name="gap")
-                nc.vector.tensor_tensor(gap[:], d_rows[t][:].indirect(entries("n2", h)), d1[:], ALU.subtract)
-                gate = ring.tile([P, HALF], F32, name="gate")
-                nc.scalar.activation(out=gate[:], in_=gap[:], func=ACT.Tanh, scale=-1.0)
-                nc.vector.scalar_tensor_tensor(
-                    z_planes[:, t, :], y_acc[t][:, cols], gain[:, t : t + 1], gate[:], ALU.mult, ALU.mult
-                )
-            z_grouped = keep.tile([P, HALF, PACK], BF16, name="z_grouped%d" % h, align_bytes=64)
-            nc.vector.tensor_copy(
-                out=z_grouped[:].rearrange("p (c i) t -> p c t i", i=4),
-                in_=z_planes[:].rearrange("p t (c i) -> p c t i", i=4),
-            )
-            z_words = keep.tile([P, HALF], U32, name="z_words%d" % h, align_bytes=64)
-            z_scales = keep.tile([P, HALF], U8, name="z_scales%d" % h, align_bytes=64)
-            nc.vector.quantize_mx(
-                out=z_words[:].bitcast(FP8X4), scales=z_scales[:], in_=z_grouped[:].rearrange("p n t -> p (n t)")
-            )
-            for t in range(PACK):
-                product(s_acc[t][:, cols], x_cand, t, (z_words, z_scales))
-                if h == 0 or t == 0:
-                    nc.scalar.activation(out=s_rows[t][:, cols], in_=s_acc[t][:, cols], func=ACT.Copy, scale=0.0625)
-                else:
-                    nc.vector.tensor_scalar(s_rows[t][:, cols], s_acc[t][:, cols], 0.0625, None, ALU.mult)
+            quantise(z_grouped[:, cols, :].rearrange("p n t -> p (n t)"), z_mx[h][0][:], z_mx[h][1][:])
 
-        out_rows = out.rearrange("(p t) c -> p t c", t=PACK)
-        for t in range(PACK):
+        def scores(t, on_scalar):
             for h in range(2):
                 cols = slice(h * HALF, (h + 1) * HALF)
-                window = s_rows[t]
-                sig = ring.tile([P, HALF], F32, name="sig")
-                nc.scalar.activation(out=sig[:], in_=window[:].indirect(entries("n3", h)), func=ACT.Sigmoid)
-                first = ring.tile([P, HALF], F32, name="first")
-                second = ring.tile([P, HALF], F32, name="second")
-                result = ring.tile([P, HALF], F32, name="result", bufs=8)
-                if 2 * t + h in SCALAR_FETCH:
-                    s4 = ring.tile([P, HALF], F32, name="s4")
-                    nc.scalar.activation(out=s4[:], in_=window[:].indirect(entries("n4", h)), func=ACT.Copy)
-                    nc.vector.tensor_tensor(first[:], s4[:], window[:, cols], ALU.subtract)
-                    nc.vector.tensor_tensor(second[:], first[:], sig[:], ALU.mult)
-                    nc.vector.tensor_tensor(result[:], second[:], window[:, cols], ALU.add)
+                acc = psum.tile([P, HALF], F32, name="s_acc%d_%d" % (t, h), tag="bank%d" % (PACK * h + t))
+                product(acc[:], x_cand, t, z_mx[h])
+                if on_scalar:
+                    nc.scalar.activation(out=windows[t][:, cols], in_=acc[:], func=ACT.Copy, scale=0.0625)
                 else:
-                    nc.vector.tensor_tensor(first[:], window[:].indirect(entries("n4", h)), sig[:], ALU.mult)
-                    nc.vector.scalar_tensor_tensor(second[:], sig[:], -1.0, window[:, cols], ALU.add, ALU.mult)
-                    nc.vector.tensor_tensor(result[:], first[:], second[:], ALU.subtract)
+                    nc.vector.tensor_scalar(windows[t][:, cols], acc[:], 0.0625, None, ALU.mult)
+
+        scores(0, True)
+        scores(1, False)
+        scores(2, False)
+
+        out_rows = out.rearrange("(p t) c -> p t c", t=PACK)
+        pending = []
+
+        def finish():
+            for t, cols, result, left, right, op in pending:
+                nc.vector.tensor_tensor(result[:], left, right, op)
                 nc.sync.dma_start(out=out_rows[:, t, cols], in_=result[:])
+            pending.clear()
+
+        for i, (t, c0, c1, scalar_fetch) in enumerate(PIECES):
+            if (t, c0) == (2, 0):
+                scores(3, True)
+            cols = slice(c0, c1)
+            window = windows[t]
+            here = window[:, cols]
+            far = window[:].indirect(lists["n4"][:, c0 // 16 : c1 // 16])
+            sig, first, second, result, s4 = [
+                keep.tile([P, c1 - c0], F32, name="%s%d" % (name, i)) for name in ("sig", "first", "second", "result", "s4_")
+            ]
+            if scalar_fetch:
+                nc.scalar.activation(out=s4[:], in_=far, func=ACT.Copy)
+            nc.scalar.activation(
+                out=sig[:], in_=window[:].indirect(lists["n3"][:, c0 // 16 : c1 // 16]), func=ACT.Sigmoid
+            )
+            if scalar_fetch:
+                nc.vector.tensor_tensor(first[:], s4[:], here, ALU.subtract)
+                finish()
+                nc.vector.tensor_tensor(second[:], first[:], sig[:], ALU.mult)
+                pending.append((t, cols, result, second[:], here, ALU.add))
+            else:
+                nc.vector.tensor_tensor(first[:], far, sig[:], ALU.mult)
+                finish()
+                nc.vector.scalar_tensor_tensor(second[:], sig[:], -1.0, here, ALU.add, ALU.mult)
+                pending.append((t, cols, result, first[:], second[:], ALU.subtract))
+        finish()

@@ -20,7 +20,7 @@ PACK = 4
 HALF = 256
 WINDOW = 1024
 GPSIMD_CHANNELS = 32
-SCALAR_WEAVE = 192
+SCALAR_LATE = (0,)
 PIECES = ((0, 0, 256, False), (0, 256, 512, False), (1, 0, 512, False), (2, 0, 512, True), (3, 0, 256, True), (3, 256, 512, True))
 
 
@@ -36,6 +36,9 @@ def tile_picked_twcjointbtrack_none_p_kernel(
         lists = {}
         for name in ("two", "offs", "n1", "n2", "cand", "n3", "n4"):
             lists[name] = keep.tile([P, S // 16], U16, name="list_" + name)
+
+        def entries(name, c0, c1):
+            return lists[name][:, c0 // 16 : c1 // 16]
 
         xw = keep.tile([P, T], U32, name="xw", align_bytes=64)
         xs = keep.tile([P, T], U8, name="xs", align_bytes=64)
@@ -66,18 +69,18 @@ def tile_picked_twcjointbtrack_none_p_kernel(
         nc.sync.dma_start(out=lists["two"][:], in_=two)
         raw2 = load_weight(w2, "w2")
         nc.sync.dma_start(out=lists["offs"][:], in_=offs)
+        nc.sync.dma_start(out=lists["cand"][:], in_=cand)
         raw1 = load_weight(w1, "w1")
         nc.sync.dma_start(out=lists["n1"][:], in_=n1)
         nc.sync.dma_start(out=lists["n2"][:], in_=n2)
-        nc.sync.dma_start(out=lists["cand"][:], in_=cand)
         nc.sync.dma_start(out=gain[:], in_=gs.rearrange("(p t) o -> p (t o)", t=PACK))
         nc.sync.dma_start(out=lists["n3"][:], in_=n3)
         nc.sync.dma_start(out=lists["n4"][:], in_=n4)
 
-        def pick(name, words, scales, dealt):
+        def pick(offsets, words, scales, dealt):
             for dst, src in ((words, xw), (scales, xs)):
                 view = dst[:].rearrange("p (t m) -> p m t", t=PACK) if dealt else dst[:]
-                nc.vector.tensor_copy(out=view, in_=src[:].indirect(lists[name][:]))
+                nc.vector.tensor_copy(out=view, in_=src[:].indirect(offsets))
             return words, scales
 
         def round_weight(on_scalar, grouped, halves, m0, m1):
@@ -109,8 +112,8 @@ def tile_picked_twcjointbtrack_none_p_kernel(
                 keep.tile([P, width], U8, name=name + "_scales", align_bytes=64),
             )
 
-        x_two = pick("two", *mx_tiles("two", S), False)
-        grouped2 = shared.tile([P, PACK, P, PACK], BF16, name="w2_bf16", align_bytes=64, offset=0)
+        x_two = pick(lists["two"][:], *mx_tiles("two", S), False)
+        grouped2 = shared.tile([P, PACK, P, PACK], BF16, name="w2_bf16", align_bytes=64, offset=64)
         round_weight(True, grouped2, raw2, 0, 64)
         round_weight(True, grouped2, raw2, 64, P - GPSIMD_CHANNELS)
         round_weight(False, grouped2, raw2, P - GPSIMD_CHANNELS, P)
@@ -119,83 +122,108 @@ def tile_picked_twcjointbtrack_none_p_kernel(
         for u in range(2):
             cols = slice(u * HALF, (u + 1) * HALF)
             quantise(flat2[:, u * PACK * HALF : (u + 1) * PACK * HALF], w2_mx[0][:, cols], w2_mx[1][:, cols])
-        x_offs = pick(
-            "offs",
-            keep.tile([P, S], U32, name="offs_words", align_bytes=64),
-            shared.tile([P, S], U8, name="offs_scales", align_bytes=64, offset=0),
-            False,
-        )
+        x_offs = [
+            pick(
+                entries("offs", 0, HALF),
+                keep.tile([P, HALF], U32, name="offs_words0", align_bytes=64),
+                shared.tile([P, HALF], U8, name="offs_scales0", align_bytes=64, offset=0),
+                False,
+            ),
+            pick(
+                entries("offs", HALF, S),
+                shared.tile([P, HALF], U32, name="offs_words1", align_bytes=64, offset=512),
+                shared.tile([P, HALF], U8, name="offs_scales1", align_bytes=64, offset=256),
+                False,
+            ),
+        ]
         x_cand = pick(
-            "cand",
-            shared.tile([P, S], U32, name="cand_words", align_bytes=64, offset=1024),
-            shared.tile([P, S], U8, name="cand_scales", align_bytes=64, offset=512),
+            lists["cand"][:],
+            shared.tile([P, S], U32, name="cand_words", align_bytes=64, offset=2048),
+            shared.tile([P, S], U8, name="cand_scales", align_bytes=64, offset=1536),
             True,
         )
         d_acc = [psum.tile([P, S], F32, name="d_acc%d" % t, tag="bank%d" % t) for t in range(PACK)]
         for t in range(PACK):
             product(d_acc[t][:], w2_mx, t, x_two)
-        grouped1 = shared.tile([P, PACK, P, PACK], BF16, name="w1_bf16", align_bytes=64, offset=3072)
+        grouped1 = shared.tile([P, PACK, P, PACK], BF16, name="w1_bf16", align_bytes=64, offset=4096)
         round_weight(False, grouped1, raw1, 0, 64)
         round_weight(False, grouped1, raw1, 64, P)
 
         y_acc = [psum.tile([P, S], F32, name="y_acc%d" % t, tag="bank%d" % (PACK + t)) for t in range(PACK)]
-        gaps = [keep.tile([P, S], F32, name="gap%d" % t) for t in range(PACK)]
-        z_planes = keep.tile([P, PACK, S], BF16, name="z_planes")
+        d_first = [keep.tile([P, S], F32, name="d_first%d" % t) for t in range(PACK)]
+        z_grouped = [keep.tile([P, HALF, PACK], BF16, name="z_grouped%d" % h, align_bytes=64) for h in range(2)]
+        z_mx = [mx_tiles("z%d" % h, HALF) for h in range(2)]
+
+        def fetch_first(t):
+            nc.scalar.activation(out=windows[t][:, :S], in_=d_acc[t][:], func=ACT.Copy)
+            nc.scalar.activation(out=d_first[t][:], in_=windows[t][:].indirect(lists["n1"][:]), func=ACT.Copy)
 
         def difference(t):
-            nc.scalar.activation(out=windows[t][:, :S], in_=d_acc[t][:], func=ACT.Copy)
-            d1 = keep.tile([P, S], F32, name="d1_%d" % t)
-            nc.scalar.activation(out=d1[:], in_=windows[t][:].indirect(lists["n1"][:]), func=ACT.Copy)
-            nc.vector.tensor_tensor(gaps[t][:], windows[t][:].indirect(lists["n2"][:]), d1[:], ALU.subtract)
+            gap = keep.tile([P, S], F32, name="gap%d" % t)
+            nc.vector.tensor_tensor(gap[:], windows[t][:].indirect(lists["n2"][:]), d_first[t][:], ALU.subtract)
+            return gap
 
-        def gated(t):
-            gate = keep.tile([P, S], F32, name="gate%d" % t)
-            nc.scalar.activation(out=gate[:], in_=gaps[t][:], func=ACT.Tanh, scale=-1.0)
-            nc.vector.scalar_tensor_tensor(
-                z_planes[:, t, :], y_acc[t][:], gain[:, t : t + 1], gate[:], ALU.mult, ALU.mult
+        def gate_of(gap, name, tag):
+            gate = keep.tile([P, gap.shape[1]], F32, name=name, tag=tag)
+            nc.scalar.activation(out=gate[:], in_=gap, func=ACT.Tanh, scale=-1.0)
+            return gate
+
+        def gated(planes, h, gates):
+            for t in range(PACK):
+                nc.vector.scalar_tensor_tensor(
+                    planes[:, t, :],
+                    y_acc[t][:, h * HALF : (h + 1) * HALF],
+                    gain[:, t : t + 1],
+                    gates[t],
+                    ALU.mult,
+                    ALU.mult,
+                )
+
+        def weave(copy, h, planes, c0, c1):
+            copy(
+                out=z_grouped[h][:, c0:c1, :].rearrange("p (c i) t -> p c t i", i=4),
+                in_=planes[:, :, c0:c1].rearrange("p t (c i) -> p c t i", i=4),
             )
 
-        difference(0)
+        def quantise_z(h):
+            quantise(z_grouped[h][:].rearrange("p n t -> p (n t)"), z_mx[h][0][:], z_mx[h][1][:])
+
+        def scores(t, h, on_scalar):
+            cols = slice(h * HALF, (h + 1) * HALF)
+            acc = psum.tile([P, HALF], F32, name="s_acc%d_%d" % (t, h), tag="bank%d" % (PACK * h + t))
+            product(acc[:], x_cand, t, z_mx[h])
+            if on_scalar:
+                nc.scalar.activation(out=windows[t][:, cols], in_=acc[:], func=ACT.Copy, scale=0.0625)
+            else:
+                nc.vector.tensor_scalar(windows[t][:, cols], acc[:], 0.0625, None, ALU.mult)
+
         w1_mx = mx_tiles("w1", H)
         quantise(grouped1[:].rearrange("p t m j -> p (t m j)"), w1_mx[0][:], w1_mx[1][:])
         for t in range(PACK):
-            product(y_acc[t][:], w1_mx, t, x_offs)
-        difference(1)
-        difference(2)
-        gated(0)
-        difference(3)
-        for t in range(1, PACK):
-            gated(t)
-
-        z_grouped = keep.tile([P, S, PACK], BF16, name="z_grouped", align_bytes=64)
-
-        def weave(copy, c0, c1):
-            copy(
-                out=z_grouped[:, c0:c1, :].rearrange("p (c i) t -> p c t i", i=4),
-                in_=z_planes[:, :, c0:c1].rearrange("p t (c i) -> p c t i", i=4),
-            )
-
-        weave(nc.scalar.copy, S - SCALAR_WEAVE, S)
-        weave(nc.vector.tensor_copy, 0, HALF)
-        weave(nc.vector.tensor_copy, HALF, S - SCALAR_WEAVE)
-        z_mx = [mx_tiles("z%d" % h, HALF) for h in range(2)]
-        for h in range(2):
-            cols = slice(h * HALF, (h + 1) * HALF)
-            quantise(z_grouped[:, cols, :].rearrange("p n t -> p (n t)"), z_mx[h][0][:], z_mx[h][1][:])
-
-        def scores(t, on_scalar):
             for h in range(2):
-                cols = slice(h * HALF, (h + 1) * HALF)
-                acc = psum.tile([P, HALF], F32, name="s_acc%d_%d" % (t, h), tag="bank%d" % (PACK * h + t))
-                product(acc[:], x_cand, t, z_mx[h])
-                if on_scalar:
-                    nc.scalar.activation(out=windows[t][:, cols], in_=acc[:], func=ACT.Copy, scale=0.0625)
-                else:
-                    nc.vector.tensor_scalar(windows[t][:, cols], acc[:], 0.0625, None, ALU.mult)
-
-        scores(0, True)
-        scores(1, False)
-        scores(2, False)
+                product(y_acc[t][:, h * HALF : (h + 1) * HALF], w1_mx, t, x_offs[h])
+        gaps = []
+        for t in range(PACK):
+            fetch_first(t)
+            gaps.append(difference(t))
+        last = PACK - 1
+        gates = [gate_of(gaps[t][:], "gate%d" % t, "gate%d" % t) for t in range(last)]
+        gate_early = gate_of(gaps[last][:, :HALF], "gate_early", "early")
+        gate_late = gate_of(gaps[last][:, HALF:], "gate_late", "late")
+        planes_early = keep.tile([P, PACK, HALF], BF16, name="planes_early")
+        gated(planes_early, 0, [g[:, :HALF] for g in gates] + [gate_early[:]])
+        weave(nc.scalar.copy, 0, planes_early, 0, HALF)
+        planes_late = keep.tile([P, PACK, HALF], BF16, name="planes_late", tag="early")
+        gated(planes_late, 1, [g[:, HALF:] for g in gates] + [gate_late[:]])
+        weave(nc.scalar.copy, 1, planes_late, 0, HALF // 2)
+        quantise_z(0)
+        weave(nc.vector.tensor_copy, 1, planes_late, HALF // 2, HALF)
+        for t in range(last):
+            scores(t, 0, True)
+        quantise_z(1)
+        scores(last, 0, False)
+        for t in range(PACK):
+            scores(t, 1, t in SCALAR_LATE)
 
         out_rows = out.rearrange("(p t) c -> p t c", t=PACK)
         pending = []
@@ -207,20 +235,17 @@ def tile_picked_twcjointbtrack_none_p_kernel(
             pending.clear()
 
         for i, (t, c0, c1, scalar_fetch) in enumerate(PIECES):
-            if (t, c0) == (2, 0):
-                scores(3, True)
             cols = slice(c0, c1)
             window = windows[t]
             here = window[:, cols]
-            far = window[:].indirect(lists["n4"][:, c0 // 16 : c1 // 16])
-            sig, first, second, result, s4 = [
-                keep.tile([P, c1 - c0], F32, name="%s%d" % (name, i)) for name in ("sig", "first", "second", "result", "s4_")
+            far = window[:].indirect(entries("n4", c0, c1))
+            sig, first, second, result = [
+                keep.tile([P, c1 - c0], F32, name="%s%d" % (name, i)) for name in ("sig", "first", "second", "result")
             ]
             if scalar_fetch:
+                s4 = keep.tile([P, c1 - c0], F32, name="s4_%d" % i)
                 nc.scalar.activation(out=s4[:], in_=far, func=ACT.Copy)
-            nc.scalar.activation(
-                out=sig[:], in_=window[:].indirect(lists["n3"][:, c0 // 16 : c1 // 16]), func=ACT.Sigmoid
-            )
+            nc.scalar.activation(out=sig[:], in_=window[:].indirect(entries("n3", c0, c1)), func=ACT.Sigmoid)
             if scalar_fetch:
                 nc.vector.tensor_tensor(first[:], s4[:], here, ALU.subtract)
                 finish()

@@ -19,9 +19,8 @@ P = 128
 PACK = 4
 HALF = 256
 WINDOW = 1024
-GPSIMD_CHANNELS = 32
-SCALAR_LATE = (0,)
-PIECES = ((0, 0, 256, False), (0, 256, 512, False), (1, 0, 512, False), (2, 0, 512, True), (3, 0, 256, True), (3, 256, 512, True))
+GPSIMD_CHANNELS = 28
+PIECES = ((0, 0, 256, False), (0, 256, 512, False), (1, 0, 256, False), (1, 256, 512, True), (2, 0, 512, True), (3, 0, 256, True), (3, 256, 384, True), (3, 384, 512, True))
 
 
 def tile_picked_twcjointbtrack_none_p_kernel(
@@ -44,6 +43,7 @@ def tile_picked_twcjointbtrack_none_p_kernel(
         xs = keep.tile([P, T], U8, name="xs", align_bytes=64)
         gain = keep.tile([P, PACK], F32, name="gain")
         nc.vector.memset(xs[:].bitcast(I32), 0)
+        nc.sync.dma_start(out=lists["two"][:], in_=two)
         nc.sync.dma_start(out=xw[:].bitcast(I32), in_=x_words[0].rearrange("p n r -> p (n r)").bitcast(I32))
         for q in range(4):
             nc.sync.dma_start(
@@ -66,7 +66,6 @@ def tile_picked_twcjointbtrack_none_p_kernel(
                 halves.append(raw)
             return halves
 
-        nc.sync.dma_start(out=lists["two"][:], in_=two)
         raw2 = load_weight(w2, "w2")
         nc.sync.dma_start(out=lists["offs"][:], in_=offs)
         nc.sync.dma_start(out=lists["cand"][:], in_=cand)
@@ -114,28 +113,20 @@ def tile_picked_twcjointbtrack_none_p_kernel(
 
         x_two = pick(lists["two"][:], *mx_tiles("two", S), False)
         grouped2 = shared.tile([P, PACK, P, PACK], BF16, name="w2_bf16", align_bytes=64, offset=64)
-        round_weight(True, grouped2, raw2, 0, 64)
-        round_weight(True, grouped2, raw2, 64, P - GPSIMD_CHANNELS)
-        round_weight(False, grouped2, raw2, P - GPSIMD_CHANNELS, P)
+        for m0 in (0, 64):
+            round_weight(True, grouped2, raw2, m0, m0 + 64 - GPSIMD_CHANNELS)
+            round_weight(False, grouped2, raw2, m0 + 64 - GPSIMD_CHANNELS, m0 + 64)
         w2_mx = mx_tiles("w2", H)
         flat2 = grouped2[:].rearrange("p t m j -> p (t m j)")
         for u in range(2):
             cols = slice(u * HALF, (u + 1) * HALF)
             quantise(flat2[:, u * PACK * HALF : (u + 1) * PACK * HALF], w2_mx[0][:, cols], w2_mx[1][:, cols])
-        x_offs = [
-            pick(
-                entries("offs", 0, HALF),
-                keep.tile([P, HALF], U32, name="offs_words0", align_bytes=64),
-                shared.tile([P, HALF], U8, name="offs_scales0", align_bytes=64, offset=0),
-                False,
-            ),
-            pick(
-                entries("offs", HALF, S),
-                shared.tile([P, HALF], U32, name="offs_words1", align_bytes=64, offset=512),
-                shared.tile([P, HALF], U8, name="offs_scales1", align_bytes=64, offset=256),
-                False,
-            ),
-        ]
+        x_offs = pick(
+            lists["offs"][:],
+            keep.tile([P, S], U32, name="offs_words", align_bytes=64),
+            shared.tile([P, S], U8, name="offs_scales", align_bytes=64, offset=1024),
+            False,
+        )
         x_cand = pick(
             lists["cand"][:],
             shared.tile([P, S], U32, name="cand_words", align_bytes=64, offset=2048),
@@ -188,20 +179,21 @@ def tile_picked_twcjointbtrack_none_p_kernel(
         def quantise_z(h):
             quantise(z_grouped[h][:].rearrange("p n t -> p (n t)"), z_mx[h][0][:], z_mx[h][1][:])
 
+        s_windows = windows[: PACK - 1] + [keep.tile([P, S], F32, name="s_last")]
+
         def scores(t, h, on_scalar):
             cols = slice(h * HALF, (h + 1) * HALF)
             acc = psum.tile([P, HALF], F32, name="s_acc%d_%d" % (t, h), tag="bank%d" % (PACK * h + t))
             product(acc[:], x_cand, t, z_mx[h])
             if on_scalar:
-                nc.scalar.activation(out=windows[t][:, cols], in_=acc[:], func=ACT.Copy, scale=0.0625)
+                nc.scalar.activation(out=s_windows[t][:, cols], in_=acc[:], func=ACT.Copy, scale=0.0625)
             else:
-                nc.vector.tensor_scalar(windows[t][:, cols], acc[:], 0.0625, None, ALU.mult)
+                nc.vector.tensor_scalar(s_windows[t][:, cols], acc[:], 0.0625, None, ALU.mult)
 
         w1_mx = mx_tiles("w1", H)
         quantise(grouped1[:].rearrange("p t m j -> p (t m j)"), w1_mx[0][:], w1_mx[1][:])
         for t in range(PACK):
-            for h in range(2):
-                product(y_acc[t][:, h * HALF : (h + 1) * HALF], w1_mx, t, x_offs[h])
+            product(y_acc[t][:], w1_mx, t, x_offs)
         gaps = []
         for t in range(PACK):
             fetch_first(t)
@@ -221,9 +213,10 @@ def tile_picked_twcjointbtrack_none_p_kernel(
         for t in range(last):
             scores(t, 0, True)
         quantise_z(1)
+        scores(0, 1, True)
         scores(last, 0, False)
-        for t in range(PACK):
-            scores(t, 1, t in SCALAR_LATE)
+        for t in range(1, PACK):
+            scores(t, 1, False)
 
         out_rows = out.rearrange("(p t) c -> p t c", t=PACK)
         pending = []
@@ -236,7 +229,7 @@ def tile_picked_twcjointbtrack_none_p_kernel(
 
         for i, (t, c0, c1, scalar_fetch) in enumerate(PIECES):
             cols = slice(c0, c1)
-            window = windows[t]
+            window = s_windows[t]
             here = window[:, cols]
             far = window[:].indirect(entries("n4", c0, c1))
             sig, first, second, result = [

from contextlib import ExitStack

import concourse.mybir as mybir

K, T, S, H, C = 512, 2048, 512, 512, 512
FLOPS = 3 * 2 * 512 * 512 * 512

F32 = mybir.dt.float32
BF16 = mybir.dt.bfloat16
I32 = mybir.dt.int32
U32 = mybir.dt.uint32
U16 = mybir.dt.uint16
U8 = mybir.dt.uint8
FP8X4 = mybir.dt.float8_e4m3fn_x4
ACT = mybir.ActivationFunctionType
ALU = mybir.AluOpType

P = 128
PACK = 4
HALF = 256
WINDOW = 1024
GPSIMD_CHANNELS = 28
PIECES = ((0, 0, 256, False), (0, 256, 512, False), (1, 0, 256, False), (1, 256, 512, True), (2, 0, 512, True), (3, 0, 256, True), (3, 256, 384, True), (3, 384, 512, True))


def tile_picked_twcjointbtrack_none_p_kernel(
    tc, x_words, x_scales, w1, w2, gs, offs, two, n1, n2, cand, n3, n4, out
):
    nc = tc.nc
    with ExitStack() as ctx:
        keep = ctx.enter_context(tc.tile_pool(name="keep", bufs=1))
        shared = ctx.enter_context(tc.tile_pool(name="shared", bufs=1))
        psum = ctx.enter_context(tc.psum_pool(name="psum", bufs=1))

        lists = {}
        for name in ("two", "offs", "n1", "n2", "cand", "n3", "n4"):
            lists[name] = keep.tile([P, S // 16], U16, name="list_" + name)

        def entries(name, c0, c1):
            return lists[name][:, c0 // 16 : c1 // 16]

        xw = keep.tile([P, T], U32, name="xw", align_bytes=64)
        xs = keep.tile([P, T], U8, name="xs", align_bytes=64)
        gain = keep.tile([P, PACK], F32, name="gain")
        nc.vector.memset(xs[:].bitcast(I32), 0)
        nc.sync.dma_start(out=lists["two"][:], in_=two)
        nc.sync.dma_start(out=xw[:].bitcast(I32), in_=x_words[0].rearrange("p n r -> p (n r)").bitcast(I32))
        for q in range(4):
            nc.sync.dma_start(
                out=xs[32 * q : 32 * q + 4, :].bitcast(I32), in_=x_scales[0, 4 * q : 4 * q + 4, :].bitcast(I32)
            )
        windows = [keep.tile([P, WINDOW], F32, name="window%d" % t) for t in range(PACK)]
        for t in range(PACK):
            nc.gpsimd.memset(windows[t][:, S:], 0.0)
        warm = keep.tile([P, 2], F32, name="warm")
        nc.gpsimd.memset(warm[:, 0:1], 0.0)
        nc.scalar.activation(out=warm[:, 1:2], in_=warm[:, 0:1], func=ACT.Sigmoid)

        def load_weight(w, name):
            halves = []
            for h in range(2):
                raw = keep.tile([P, PACK, HALF], F32, name="%s_raw%d" % (name, h))
                nc.sync.dma_start(
                    out=raw[:], in_=w.rearrange("(p j) c -> p j c", j=PACK)[:, :, h * HALF : (h + 1) * HALF]
                )
                halves.append(raw)
            return halves

        raw2 = load_weight(w2, "w2")
        nc.sync.dma_start(out=lists["offs"][:], in_=offs)
        nc.sync.dma_start(out=lists["cand"][:], in_=cand)
        raw1 = load_weight(w1, "w1")
        nc.sync.dma_start(out=lists["n1"][:], in_=n1)
        nc.sync.dma_start(out=lists["n2"][:], in_=n2)
        nc.sync.dma_start(out=gain[:], in_=gs.rearrange("(p t) o -> p (t o)", t=PACK))
        nc.sync.dma_start(out=lists["n3"][:], in_=n3)
        nc.sync.dma_start(out=lists["n4"][:], in_=n4)

        def pick(offsets, words, scales, dealt):
            for dst, src in ((words, xw), (scales, xs)):
                view = dst[:].rearrange("p (t m) -> p m t", t=PACK) if dealt else dst[:]
                nc.vector.tensor_copy(out=view, in_=src[:].indirect(offsets))
            return words, scales

        def round_weight(on_scalar, grouped, halves, m0, m1):
            h, base = divmod(m0, HALF // PACK)
            dst = grouped[:, :, m0:m1, :].rearrange("p t m j -> p m t j")
            src = halves[h][:].rearrange("p j (m t) -> p m t j", t=PACK)[:, base : base + m1 - m0]
            if on_scalar:
                nc.scalar.activation(out=dst, in_=src, func=ACT.Copy)
            else:
                nc.gpsimd.tensor_scalar(dst, src, 1.0, 0.0, ALU.mult, ALU.add)

        def quantise(flat, words, scales):
            nc.vector.quantize_mx(out=words.bitcast(FP8X4), scales=scales, in_=flat)

        def product(acc, stationary, t, moving):
            nc.tensor.matmul_mx(
                out=acc,
                lhsT=stationary[0][:, t * P : (t + 1) * P].bitcast(FP8X4),
                lhsT_scale=stationary[1][:, t * P : (t + 1) * P],
                rhs=moving[0][:].bitcast(FP8X4),
                rhs_scale=moving[1][:],
                start=True,
                stop=True,
            )

        def mx_tiles(name, width):
            return (
                keep.tile([P, width], U32, name=name + "_words", align_bytes=64),
                keep.tile([P, width], U8, name=name + "_scales", align_bytes=64),
            )

        x_two = pick(lists["two"][:], *mx_tiles("two", S), False)
        grouped2 = shared.tile([P, PACK, P, PACK], BF16, name="w2_bf16", align_bytes=64, offset=64)
        for m0 in (0, 64):
            round_weight(True, grouped2, raw2, m0, m0 + 64 - GPSIMD_CHANNELS)
            round_weight(False, grouped2, raw2, m0 + 64 - GPSIMD_CHANNELS, m0 + 64)
        w2_mx = mx_tiles("w2", H)
        flat2 = grouped2[:].rearrange("p t m j -> p (t m j)")
        for u in range(2):
            cols = slice(u * HALF, (u + 1) * HALF)
            quantise(flat2[:, u * PACK * HALF : (u + 1) * PACK * HALF], w2_mx[0][:, cols], w2_mx[1][:, cols])
        x_offs = pick(
            lists["offs"][:],
            keep.tile([P, S], U32, name="offs_words", align_bytes=64),
            shared.tile([P, S], U8, name="offs_scales", align_bytes=64, offset=1024),
            False,
        )
        x_cand = pick(
            lists["cand"][:],
            shared.tile([P, S], U32, name="cand_words", align_bytes=64, offset=2048),
            shared.tile([P, S], U8, name="cand_scales", align_bytes=64, offset=1536),
            True,
        )
        d_acc = [psum.tile([P, S], F32, name="d_acc%d" % t, tag="bank%d" % t) for t in range(PACK)]
        for t in range(PACK):
            product(d_acc[t][:], w2_mx, t, x_two)
        grouped1 = shared.tile([P, PACK, P, PACK], BF16, name="w1_bf16", align_bytes=64, offset=4096)
        round_weight(False, grouped1, raw1, 0, 64)
        round_weight(False, grouped1, raw1, 64, P)

        y_acc = [psum.tile([P, S], F32, name="y_acc%d" % t, tag="bank%d" % (PACK + t)) for t in range(PACK)]
        d_first = [keep.tile([P, S], F32, name="d_first%d" % t) for t in range(PACK)]
        z_grouped = [keep.tile([P, HALF, PACK], BF16, name="z_grouped%d" % h, align_bytes=64) for h in range(2)]
        z_mx = [mx_tiles("z%d" % h, HALF) for h in range(2)]

        def fetch_first(t):
            nc.scalar.activation(out=windows[t][:, :S], in_=d_acc[t][:], func=ACT.Copy)
            nc.scalar.activation(out=d_first[t][:], in_=windows[t][:].indirect(lists["n1"][:]), func=ACT.Copy)

        def difference(t):
            gap = keep.tile([P, S], F32, name="gap%d" % t)
            nc.vector.tensor_tensor(gap[:], windows[t][:].indirect(lists["n2"][:]), d_first[t][:], ALU.subtract)
            return gap

        def gate_of(gap, name, tag):
            gate = keep.tile([P, gap.shape[1]], F32, name=name, tag=tag)
            nc.scalar.activation(out=gate[:], in_=gap, func=ACT.Tanh, scale=-1.0)
            return gate

        def gated(planes, h, gates):
            for t in range(PACK):
                nc.vector.scalar_tensor_tensor(
                    planes[:, t, :],
                    y_acc[t][:, h * HALF : (h + 1) * HALF],
                    gain[:, t : t + 1],
                    gates[t],
                    ALU.mult,
                    ALU.mult,
                )

        def weave(copy, h, planes, c0, c1):
            copy(
                out=z_grouped[h][:, c0:c1, :].rearrange("p (c i) t -> p c t i", i=4),
                in_=planes[:, :, c0:c1].rearrange("p t (c i) -> p c t i", i=4),
            )

        def quantise_z(h):
            quantise(z_grouped[h][:].rearrange("p n t -> p (n t)"), z_mx[h][0][:], z_mx[h][1][:])

        s_windows = windows[: PACK - 1] + [keep.tile([P, S], F32, name="s_last")]

        def scores(t, h, on_scalar):
            cols = slice(h * HALF, (h + 1) * HALF)
            acc = psum.tile([P, HALF], F32, name="s_acc%d_%d" % (t, h), tag="bank%d" % (PACK * h + t))
            product(acc[:], x_cand, t, z_mx[h])
            if on_scalar:
                nc.scalar.activation(out=s_windows[t][:, cols], in_=acc[:], func=ACT.Copy, scale=0.0625)
            else:
                nc.vector.tensor_scalar(s_windows[t][:, cols], acc[:], 0.0625, None, ALU.mult)

        w1_mx = mx_tiles("w1", H)
        quantise(grouped1[:].rearrange("p t m j -> p (t m j)"), w1_mx[0][:], w1_mx[1][:])
        for t in range(PACK):
            product(y_acc[t][:], w1_mx, t, x_offs)
        gaps = []
        for t in range(PACK):
            fetch_first(t)
            gaps.append(difference(t))
        last = PACK - 1
        gates = [gate_of(gaps[t][:], "gate%d" % t, "gate%d" % t) for t in range(last)]
        gate_early = gate_of(gaps[last][:, :HALF], "gate_early", "early")
        gate_late = gate_of(gaps[last][:, HALF:], "gate_late", "late")
        planes_early = keep.tile([P, PACK, HALF], BF16, name="planes_early")
        gated(planes_early, 0, [g[:, :HALF] for g in gates] + [gate_early[:]])
        weave(nc.scalar.copy, 0, planes_early, 0, HALF)
        planes_late = keep.tile([P, PACK, HALF], BF16, name="planes_late", tag="early")
        gated(planes_late, 1, [g[:, HALF:] for g in gates] + [gate_late[:]])
        weave(nc.scalar.copy, 1, planes_late, 0, HALF // 2)
        quantise_z(0)
        weave(nc.vector.tensor_copy, 1, planes_late, HALF // 2, HALF)
        for t in range(last):
            scores(t, 0, True)
        quantise_z(1)
        scores(0, 1, True)
        scores(last, 0, False)
        for t in range(1, PACK):
            scores(t, 1, False)

        out_rows = out.rearrange("(p t) c -> p t c", t=PACK)
        pending = []

        def finish():
            for t, cols, result, left, right, op in pending:
                nc.vector.tensor_tensor(result[:], left, right, op)
                nc.sync.dma_start(out=out_rows[:, t, cols], in_=result[:])
            pending.clear()

        for i, (t, c0, c1, scalar_fetch) in enumerate(PIECES):
            cols = slice(c0, c1)
            window = s_windows[t]
            here = window[:, cols]
            far = window[:].indirect(entries("n4", c0, c1))
            sig, first, second, result = [
                keep.tile([P, c1 - c0], F32, name="%s%d" % (name, i)) for name in ("sig", "first", "second", "result")
            ]
            if scalar_fetch:
                s4 = keep.tile([P, c1 - c0], F32, name="s4_%d" % i)
                nc.scalar.activation(out=s4[:], in_=far, func=ACT.Copy)
            nc.scalar.activation(out=sig[:], in_=window[:].indirect(entries("n3", c0, c1)), func=ACT.Sigmoid)
            if scalar_fetch:
                nc.vector.tensor_tensor(first[:], s4[:], here, ALU.subtract)
                finish()
                nc.vector.tensor_tensor(second[:], first[:], sig[:], ALU.mult)
                pending.append((t, cols, result, second[:], here, ALU.add))
            else:
                nc.vector.tensor_tensor(first[:], far, sig[:], ALU.mult)
                finish()
                nc.vector.scalar_tensor_tensor(second[:], sig[:], -1.0, here, ALU.add, ALU.mult)
                pending.append((t, cols, result, first[:], second[:], ALU.subtract))
        finish()
